import numpy as np
import ml_dtypes


def mxq(x, axis, fmt="e4m3"):
    dtype, down = {"e4m3": (ml_dtypes.float8_e4m3fn, 7), "e5m2": (ml_dtypes.float8_e5m2, 14)}[fmt]
    v = np.moveaxis(np.asarray(x, np.float32).astype(ml_dtypes.bfloat16).astype(np.float64), axis, -1)
    blocks = v.reshape(v.shape[:-1] + (-1, 32))
    amax = np.abs(blocks).max(-1, keepdims=True)
    byte = np.maximum(np.where(amax > 0, np.frexp(amax)[1] - 1 + 127, 0) - down, 1)
    scale = np.exp2(byte - 127.0)
    codes = (blocks / scale).astype(np.float32).astype(dtype).astype(np.float64)
    return np.moveaxis((codes * scale).reshape(v.shape), -1, axis)


WIDE = False


def mx_kscale(k):
    if not WIDE:
        return np.ones(k)
    levels = np.array([10, -10, 5, -5, 0])
    if k % 512:
        return np.exp2(np.random.permutation(np.resize(levels, k // 32))).repeat(32)
    a = np.empty((k // 512, 16))
    for p in range(k // 512):
        a[p, :8] = np.random.permutation(np.resize(levels, 8))
        for g in range(8):
            far = levels[np.abs(levels - a[p, g]) >= 10]
            a[p, g + 8] = far[np.random.randint(len(far))]
    return np.exp2(a.ravel()).repeat(32)


def f64(x):
    return np.asarray(x).astype(np.float64)


def striped(idx):
    return np.tile(idx.reshape(-1, 16).T, (8, 1)).astype(np.uint16)


def unstriped(offs):
    return offs[:16].T.reshape(-1).astype(np.int64)


E2M1 = np.array([0.0, 0.5, 1.0, 1.5, 2.0, 3.0, 4.0, 6.0, -0.0, -0.5, -1.0, -1.5, -2.0, -3.0, -4.0, -6.0])


def pack_weight(w, fmt):
    k, n = w.shape
    w = f64(np.asarray(w, np.float32).astype(ml_dtypes.bfloat16)).reshape(k // 32, 32, n)
    amax = np.abs(w).max(1)
    if fmt == "e4m3":
        byte = np.frexp(amax)[1] - 1 + 127 - 7
    else:
        mant, ex = np.frexp(amax / 6.0)
        byte = np.where(mant > 0.5, ex, ex - 1) + 127
    byte = np.clip(np.where(amax > 0, byte, 1), 1, 254)
    scaled = (w * np.exp2(127.0 - byte)[:, None, :]).reshape(k, n).astype(np.float32)
    by_word = np.ascontiguousarray(scaled.reshape(k // 512, 128, 4, n).transpose(0, 1, 3, 2))
    if fmt == "e4m3":
        words = by_word.astype(ml_dtypes.float8_e4m3fn).view(np.uint8)
    else:
        c = by_word.astype(ml_dtypes.float4_e2m1fn).view(np.uint8) & 0xF
        words = (c[..., 0::2] | (c[..., 1::2] << 4)).reshape(k // 512, 128, 2 * n)
    return np.ascontiguousarray(words), np.ascontiguousarray(byte.astype(np.uint8).reshape(k // 512, 16, n))


def unpack_weight(words, scales, fmt):
    g, _, n = scales.shape
    words = np.ascontiguousarray(words).reshape(g, 128, n, -1)
    if fmt == "e4m3":
        vals = words.view(ml_dtypes.float8_e4m3fn).astype(np.float64)
    else:
        nib = np.empty((g, 128, n, 4), np.uint8)
        nib[..., 0::2] = words & 0xF
        nib[..., 1::2] = words >> 4
        vals = E2M1[nib]
    vals = vals * np.repeat(np.exp2(scales.astype(np.float64) - 127.0), 8, axis=1)[..., None]
    return vals.transpose(0, 1, 3, 2).reshape(g * 512, n)


def gelu(v):
    return 0.5 * v * (1.0 + np.tanh(np.sqrt(2.0 / np.pi) * (v + 0.044715 * v**3)))


K, T, S, S2 = 1024, 2048, 512, 1024

def setup_inputs():
    n = np.random.standard_normal
    d = {}
    s = mx_kscale(K)[:, None]
    d["tab_words"], d["tab_scales"] = pack_weight(n((K, T)) * s, "e4m3")
    d["w1"] = (0.5 * n((K, K)) / K / s / s.T).astype(np.float32)
    d["w4_words"], d["w4_scales"] = pack_weight(0.5 * n((K, K)) / K / s / s.T, "e2m1")
    d["gain"] = (1.5 * n(S2)).astype(np.float32)
    d["route"] = (0.7 * n((S2, S))).astype(np.float32)
    d["offs"] = striped(np.random.permutation(T)[:S])
    d["offs2"] = striped(np.random.permutation(T)[:S2])
    return d

def reference(tab_words, tab_scales, w1, w4_words, w4_scales, gain, route, offs, offs2):
    TW = unpack_weight(tab_words, tab_scales, "e4m3")
    v = TW[:, unstriped(offs)]
    v2 = TW[:, unstriped(offs2)]
    a = mxq(f64(w1), 0, "e4m3").T @ v
    b = unpack_weight(w4_words, w4_scales, "e2m1").T @ v
    h = np.minimum(a, b)
    e = v2.T @ mxq(h, 0, "e4m3")
    near = np.sin(e) * f64(gain)[:, None]
    far = np.cos(e) * f64(route)
    return near + far

@@ -1,0 +1,299 @@
+import math
+from contextlib import ExitStack
+
+import concourse.mybir as mybir
+from concourse.masks import make_identity
+
+K, T, S, S2 = 1024, 2048, 512, 1024
+FLOPS = 2 * K * K * S * 2 + 2 * K * S2 * S
+
+F32 = mybir.dt.float32
+BF16 = mybir.dt.bfloat16
+I32 = mybir.dt.int32
+U32 = mybir.dt.uint32
+U16 = mybir.dt.uint16
+U8 = mybir.dt.uint8
+FP8X4 = mybir.dt.float8_e4m3fn_x4
+FP4X4 = mybir.dt.float4_e2m1fn_x4
+ALU = mybir.AluOpType
+ACT = mybir.ActivationFunctionType
+
+P = 128
+PASS = 512
+PASSES = K // PASS
+JT = S // P
+MT = S2 // P
+TURNS = 16.0
+SPLIT = 288
+TWO_PI = 2.0 * math.pi
+
+
+def tile_list_harness_crosstalk_match_kernel(
+    tc, tab_words, tab_scales, w1, w4_words, w4_scales, gain, route, offs, offs2, out
+):
+    nc = tc.nc
+    with ExitStack() as ctx:
+        lists = ctx.enter_context(tc.tile_pool(name="lists", bufs=1))
+        keep = ctx.enter_context(tc.tile_pool(name="keep", bufs=1))
+        ring = ctx.enter_context(tc.tile_pool(name="ring", bufs=5))
+        psum = ctx.enter_context(tc.psum_pool(name="psum", bufs=4))
+
+        def held(name, shape, dtype):
+            return keep.tile(shape, dtype, name=name, align_bytes=64)
+
+        idx = lists.tile([P, S // 16], U16, name="idx")
+        idx2 = lists.tile([P, S2 // 16], U16, name="idx2")
+        tab_s = held("tab_s", [P, T], U8)
+        tab_w = [held("tab_w%d" % a, [P, T], I32) for a in range(PASSES)]
+        w4_w = held("w4_w", [P, PASSES, 2 * K], U8)
+        w4_s = held("w4_s", [P, PASSES, K], U8)
+        v_w = [held("v_w%d" % a, [P, S], U32) for a in range(PASSES)]
+        v_s = held("v_s", [P, S], U8)
+        v_s1 = held("v_s1", [P, S], U8)
+        v2_w = {}
+        v2_s = held("v2_s", [P, S2], U8)
+        raw = {}
+        w1_bf = {}
+        w1_w = {}
+        w1_s = {}
+        for blk in range(PASSES):
+            for a in range(PASSES):
+                w1_bf[blk, a] = keep.tile(
+                    [P, 4 * PASS], BF16, name="w1_bf%d%d" % (blk, a), tag="shared%d%d" % (blk, a), align_bytes=64
+                )
+                w1_w[blk, a] = held("w1_w%d%d" % (blk, a), [P, PASS], U32)
+                w1_s[blk, a] = held("w1_s%d%d" % (blk, a), [P, PASS], U8)
+        route_sb = {}
+        ident = held("ident", [P, P], F32)
+        gain_rows = held("gain_rows", [P, P], F32)
+        gain_sb = held("gain_sb", [P, MT], F32)
+        one = held("one", [P, 1], F32)
+        bias_sin = held("bias_sin", [P, 1], F32)
+        bias_cos = held("bias_cos", [P, 1], F32)
+        bias_turns = held("bias_turns", [P, 1], F32)
+
+        nc.vector.memset(tab_s[:].bitcast(I32), 0)
+        nc.vector.memset(w4_s[:].rearrange("p a c -> p (a c)").bitcast(I32), 0)
+        nc.vector.memset(v_s1[:].bitcast(I32), 0)
+        for q in range(4):
+            nc.gpsimd.dma_start(
+                out=w4_s[32 * q : 32 * q + 4, :, :].bitcast(I32),
+                in_=w4_scales[:, 4 * q : 4 * q + 4, :].rearrange("a r c -> r a c").bitcast(I32),
+            )
+        nc.gpsimd.memset(gain_rows[:], 0.0)
+        make_identity(nc, ident[:])
+        nc.gpsimd.memset(one[:], 1.0)
+        nc.gpsimd.memset(bias_turns[:], TURNS)
+        nc.gpsimd.tensor_scalar(bias_sin[:], one[:], TWO_PI * TURNS, 0.0, ALU.mult, ALU.add)
+        nc.gpsimd.tensor_scalar(bias_cos[:], one[:], 0.5 * math.pi, 0.0, ALU.mult, ALU.add)
+
+        def load_w1(blk, a):
+            rows = w1[a * PASS : (a + 1) * PASS, blk * PASS : (blk + 1) * PASS]
+            raw[blk, a] = keep.tile([P, 4, PASS], F32, name="raw", tag="stream", bufs=2)
+            nc.sync.dma_start(out=raw[blk, a][:], in_=rows.rearrange("(p j) c -> p j c", j=4))
+
+        def load_tab(a):
+            nc.sync.dma_start(out=tab_w[a][:], in_=tab_words[a].rearrange("p t i -> p (t i)").bitcast(I32))
+
+        def cast_w1(copy, blk, a, first, last):
+            copy(
+                out=w1_bf[blk, a][:, 4 * first : 4 * last].rearrange("p (c i j) -> p c j i", i=4, j=4),
+                in_=raw[blk, a][:, :, first:last].rearrange("p j (c i) -> p c j i", i=4),
+            )
+
+        def quant_w1(blk, a):
+            nc.vector.quantize_mx(out=w1_w[blk, a][:].bitcast(FP8X4), scales=w1_s[blk, a][:], in_=w1_bf[blk, a][:])
+
+        def gather_words(dst, a, offsets):
+            nc.vector.tensor_copy(dst, tab_w[a][:].bitcast(U32).indirect(offsets))
+
+        nc.sync.dma_start(idx[:], offs)
+        for q in range(4):
+            nc.sync.dma_start(
+                out=tab_s[32 * q : 32 * q + 8, :].bitcast(I32),
+                in_=tab_scales[:, 4 * q : 4 * q + 4, :].bitcast(I32),
+            )
+        nc.sync.dma_start(idx2[:], offs2)
+        load_w1(0, 0)
+        load_tab(0)
+        load_w1(0, 1)
+        nc.vector.tensor_copy(v_s[:], tab_s[:].indirect(idx[:]))
+        for q in range(4):
+            nc.scalar.dma_start(
+                out=v_s1[32 * q : 32 * q + 4, :].bitcast(I32), in_=v_s[32 * q + 4 : 32 * q + 8, :].bitcast(I32)
+            )
+        load_tab(1)
+        nc.sync.dma_start(
+            out=w4_w[:].bitcast(I32), in_=w4_words.rearrange("a p c -> p a c").bitcast(I32)
+        )
+        nc.sync.dma_start(out=gain_rows[0:MT, :], in_=gain.rearrange("(b p) -> b p", p=P))
+
+        def load_route(q):
+            route_sb[q] = keep.tile([P, 4, S], F32, name="route_sb", tag="stream", bufs=2)
+            nc.sync.dma_start(
+                out=route_sb[q][:], in_=route[4 * q * P : (4 * q + 4) * P, :].rearrange("(b p) j -> p b j", p=P)
+            )
+
+        def gather_victims(a, half):
+            tag = "shared%d1" % half if a == 1 else "v2_w0%d" % half
+            v2_w[a, half] = keep.tile([P, S2 // 2], U32, name="v2_w%d%d" % (a, half), tag=tag, align_bytes=64)
+            gather_words(v2_w[a, half][:], a, idx2[:, half * S2 // 32 : (half + 1) * S2 // 32])
+
+        def gather_victim_scales(half):
+            nc.vector.tensor_copy(
+                v2_s[:, half * S2 // 2 : (half + 1) * S2 // 2],
+                tab_s[:].indirect(idx2[:, half * S2 // 32 : (half + 1) * S2 // 32]),
+            )
+
+        gather_victim_scales(0)
+        gather_victim_scales(1)
+        cast_w1(nc.scalar.copy, 0, 0, 0, PASS)
+        load_w1(1, 0)
+        gather_words(v_w[0][:], 0, idx[:])
+        gather_victims(0, 0)
+        quant_w1(0, 0)
+        gather_victims(0, 1)
+        cast_w1(nc.scalar.copy, 0, 1, 0, PASS)
+        load_w1(1, 1)
+        gather_words(v_w[1][:], 1, idx[:])
+        quant_w1(0, 1)
+
+        v_planes = [v_s, v_s1]
+        parked = {}
+        h_t = {}
+
+        def product(bank, weight, blk, jt, a, first):
+            cols = slice(jt * P, (jt + 1) * P)
+            if weight == "w4":
+                rhs = w4_w[:, a, 2 * blk * PASS : 2 * (blk + 1) * PASS].bitcast(FP4X4)
+                rhs_scale = w4_s[:, a, blk * PASS : (blk + 1) * PASS]
+            else:
+                rhs = w1_w[blk, a][:].bitcast(FP8X4)
+                rhs_scale = w1_s[blk, a][:]
+            nc.tensor.matmul_mx(
+                out=bank[:],
+                lhsT=v_w[a][:, cols].bitcast(FP8X4),
+                lhsT_scale=v_planes[a][:, cols] if weight == "w4" else v_s[4 * a : P, cols],
+                rhs=rhs,
+                rhs_scale=rhs_scale,
+                start=first,
+                stop=not first,
+            )
+
+        def park(weight, blk):
+            for jt in range(JT):
+                bank = psum.tile([P, PASS], F32, name="bank", tag="g")
+                product(bank, weight, blk, jt, 1, True)
+                product(bank, weight, blk, jt, 0, False)
+                parked[blk, jt] = held("parked%d%d" % (blk, jt), [P, PASS], F32)
+                nc.scalar.copy(
+                    out=parked[blk, jt][:].rearrange("j (u p e) -> j u p e", u=2, e=2),
+                    in_=bank[:].rearrange("j (p u e) -> j u p e", u=2, e=2),
+                )
+
+        def meet(weight, blk):
+            banks = [psum.tile([P, PASS], F32, name="abank", tag="a") for jt in range(JT)]
+            for a in range(PASSES):
+                for jt in range(JT):
+                    product(banks[jt], weight, blk, jt, a, a == 0)
+            for jt in range(JT):
+                h_t[blk, jt] = held("h_t%d%d" % (blk, jt), [P, PASS], BF16)
+                nc.vector.tensor_tensor(
+                    out=h_t[blk, jt][:].rearrange("j (u p e) -> j u p e", u=2, e=2),
+                    in0=banks[jt][:].rearrange("j (p u e) -> j u p e", u=2, e=2),
+                    in1=parked[blk, jt][:].rearrange("j (u p e) -> j u p e", u=2, e=2),
+                    op=ALU.min,
+                )
+
+        h_w = [held("h_w%d" % a, [P, S], U32) for a in range(PASSES)]
+        h_s = [held("h_s%d" % a, [P, S], U8) for a in range(PASSES)]
+        h_bf = [held("h_bf%d" % a, [P, 4 * S], BF16) for a in range(PASSES)]
+
+        def turn_h(blk):
+            words_out = h_bf[blk][:].bitcast(F32)
+            for half in range(2):
+                bank = psum.tile([P, 2, 2, P], F32, name="tbank", tag="g")
+                for s in range(2):
+                    words = h_t[blk, 2 * half + s][:].bitcast(F32)
+                    for u in range(2):
+                        nc.tensor.transpose(bank[:, s, u, :], words[:, u * P : (u + 1) * P], ident[:])
+                nc.scalar.copy(
+                    out=words_out[:, half * PASS : (half + 1) * PASS].rearrange("p (s j u) -> p s j u", s=2, u=2),
+                    in_=bank[:].rearrange("p s u j -> p s j u"),
+                )
+
+        def quant_h(blk):
+            nc.vector.quantize_mx(out=h_w[blk][:].bitcast(FP8X4), scales=h_s[blk][:], in_=h_bf[blk][:])
+
+        park("w1", 0)
+        gather_victims(1, 0)
+        meet("w4", 0)
+        park("w4", 1)
+        cast_w1(nc.vector.tensor_copy, 1, 0, 0, PASS)
+        load_route(0)
+        quant_w1(1, 0)
+        cast_w1(nc.vector.tensor_copy, 1, 1, 0, SPLIT)
+        cast_w1(nc.scalar.copy, 1, 1, SPLIT, PASS)
+        load_route(1)
+        quant_w1(1, 1)
+        gather_victims(1, 1)
+        turn_h(0)
+        quant_h(0)
+        meet("w1", 1)
+        turn_h(1)
+        gbank = psum.tile([P, PASS], F32, name="gbank", tag="g")
+        nc.tensor.transpose(gbank[:, 0:P], gain_rows[:], ident[:])
+        nc.scalar.copy(out=gain_sb[:], in_=gbank[:, 0:MT])
+        quant_h(1)
+
+        stage = {}
+
+        def match(i):
+            e = psum.tile([P, S], F32, name="e", tag="a" if i % 2 else "g")
+            cols = slice(i * P, (i + 1) * P)
+            for a in range(PASSES):
+                nc.tensor.matmul_mx(
+                    out=e[:],
+                    lhsT=v2_w[a, i // 4][:, (i % 4) * P : (i % 4 + 1) * P].bitcast(FP8X4),
+                    lhsT_scale=v2_s[4 * a : P, cols],
+                    rhs=h_w[a][:].bitcast(FP8X4),
+                    rhs_scale=h_s[a][:],
+                    start=(a == 0),
+                    stop=(a == PASSES - 1),
+                )
+            whole = ring.tile([P, S], I32, name="whole")
+            if i < 6:
+                nc.scalar.activation(out=whole[:].bitcast(U32), in_=e[:], func=ACT.Copy, scale=1.0 / TWO_PI, bias=TURNS)
+            else:
+                nc.vector.tensor_scalar(whole[:], e[:], 1.0 / TWO_PI, TURNS, ALU.mult, ALU.add)
+            stage[i] = (e, whole)
+
+        def reduce_angle(i):
+            e, whole = stage[i]
+            frac = ring.tile([P, S], F32, name="frac")
+            nc.vector.scalar_tensor_tensor(frac[:], e[:], 1.0 / TWO_PI, whole[:], ALU.mult, ALU.subtract)
+            size = ring.tile([P, S], F32, name="size")
+            cos_e = ring.tile([P, S], F32, name="cos_e")
+            sin_e = ring.tile([P, S], F32, name="sin_e")
+            nc.scalar.activation(out=size[:], in_=frac[:], func=ACT.Abs, bias=bias_turns[:])
+            nc.scalar.activation(out=sin_e[:], in_=frac[:], func=ACT.Sin, scale=TWO_PI, bias=bias_sin[:])
+            nc.scalar.activation(out=cos_e[:], in_=size[:], func=ACT.Sin, scale=-TWO_PI, bias=bias_cos[:])
+            stage[i] = (sin_e, cos_e)
+
+        def route_far(i):
+            sin_e, cos_e = stage[i]
+            far = ring.tile([P, S], F32, name="far")
+            nc.vector.tensor_tensor(out=far[:], in0=cos_e[:], in1=route_sb[i // 4][:, i % 4, :], op=ALU.mult)
+            stage[i] = (sin_e, far)
+
+        def finish(i):
+            sin_e, far = stage[i]
+            result = ring.tile([P, S], F32, name="result")
+            nc.vector.scalar_tensor_tensor(result[:], sin_e[:], gain_sb[:, i : i + 1], far[:], ALU.mult, ALU.add)
+            nc.sync.dma_start(out=out[i * P : (i + 1) * P, :], in_=result[:])
+
+        steps = ((match, 0), (reduce_angle, 1), (route_far, 2), (finish, 3))
+        for tick in range(MT + 4):
+            for step, lag in reversed(steps):
+                if 0 <= tick - lag < MT:
+                    step(tick - lag)

@@ -24,7 +24,8 @@ PASSES = K // PASS
 JT = S // P
 MT = S2 // P
 TURNS = 16.0
-SPLIT = 288
+CHUNK = 4 * PASS * 4
+ON_SCALAR = (0, 1, 2, 3)
 TWO_PI = 2.0 * math.pi
 
 
@@ -35,6 +36,7 @@ def tile_list_harness_crosstalk_match_kernel(
     with ExitStack() as ctx:
         lists = ctx.enter_context(tc.tile_pool(name="lists", bufs=1))
         keep = ctx.enter_context(tc.tile_pool(name="keep", bufs=1))
+        stream = ctx.enter_context(tc.tile_pool(name="stream", bufs=1))
         ring = ctx.enter_context(tc.tile_pool(name="ring", bufs=5))
         psum = ctx.enter_context(tc.psum_pool(name="psum", bufs=4))
 
@@ -43,7 +45,7 @@ def tile_list_harness_crosstalk_match_kernel(
 
         idx = lists.tile([P, S // 16], U16, name="idx")
         idx2 = lists.tile([P, S2 // 16], U16, name="idx2")
-        tab_s = held("tab_s", [P, T], U8)
+        tab_s = stream.tile([P, T], U8, name="tab_s", offset=CHUNK - T // 2)
         tab_w = [held("tab_w%d" % a, [P, T], I32) for a in range(PASSES)]
         w4_w = held("w4_w", [P, PASSES, 2 * K], U8)
         w4_s = held("w4_s", [P, PASSES, K], U8)
@@ -58,9 +60,8 @@ def tile_list_harness_crosstalk_match_kernel(
         w1_s = {}
         for blk in range(PASSES):
             for a in range(PASSES):
-                w1_bf[blk, a] = keep.tile(
-                    [P, 4 * PASS], BF16, name="w1_bf%d%d" % (blk, a), tag="shared%d%d" % (blk, a), align_bytes=64
-                )
+                tag = "w1_bf%d%d" % (blk, a)
+                w1_bf[blk, a] = keep.tile([P, 4 * PASS], BF16, name="w1_bf%d%d" % (blk, a), tag=tag, align_bytes=64)
                 w1_w[blk, a] = held("w1_w%d%d" % (blk, a), [P, PASS], U32)
                 w1_s[blk, a] = held("w1_s%d%d" % (blk, a), [P, PASS], U8)
         route_sb = {}
@@ -75,22 +76,18 @@ def tile_list_harness_crosstalk_match_kernel(
         nc.vector.memset(tab_s[:].bitcast(I32), 0)
         nc.vector.memset(w4_s[:].rearrange("p a c -> p (a c)").bitcast(I32), 0)
         nc.vector.memset(v_s1[:].bitcast(I32), 0)
-        for q in range(4):
-            nc.gpsimd.dma_start(
-                out=w4_s[32 * q : 32 * q + 4, :, :].bitcast(I32),
-                in_=w4_scales[:, 4 * q : 4 * q + 4, :].rearrange("a r c -> r a c").bitcast(I32),
-            )
         nc.gpsimd.memset(gain_rows[:], 0.0)
+        nc.gpsimd.dma_start(out=gain_rows[0:MT, :], in_=gain.rearrange("(b p) -> b p", p=P))
         make_identity(nc, ident[:])
         nc.gpsimd.memset(one[:], 1.0)
         nc.gpsimd.memset(bias_turns[:], TURNS)
         nc.gpsimd.tensor_scalar(bias_sin[:], one[:], TWO_PI * TURNS, 0.0, ALU.mult, ALU.add)
         nc.gpsimd.tensor_scalar(bias_cos[:], one[:], 0.5 * math.pi, 0.0, ALU.mult, ALU.add)
 
-        def load_w1(blk, a):
+        def load_w1(blk, a, tile):
             rows = w1[a * PASS : (a + 1) * PASS, blk * PASS : (blk + 1) * PASS]
-            raw[blk, a] = keep.tile([P, 4, PASS], F32, name="raw", tag="stream", bufs=2)
-            nc.sync.dma_start(out=raw[blk, a][:], in_=rows.rearrange("(p j) c -> p j c", j=4))
+            raw[blk, a] = tile
+            nc.sync.dma_start(out=tile, in_=rows.rearrange("(p j) c -> p j c", j=4))
 
         def load_tab(a):
             nc.sync.dma_start(out=tab_w[a][:], in_=tab_words[a].rearrange("p t i -> p (t i)").bitcast(I32))
@@ -114,28 +111,28 @@ def tile_list_harness_crosstalk_match_kernel(
                 in_=tab_scales[:, 4 * q : 4 * q + 4, :].bitcast(I32),
             )
         nc.sync.dma_start(idx2[:], offs2)
-        load_w1(0, 0)
         load_tab(0)
-        load_w1(0, 1)
-        nc.vector.tensor_copy(v_s[:], tab_s[:].indirect(idx[:]))
-        for q in range(4):
-            nc.scalar.dma_start(
-                out=v_s1[32 * q : 32 * q + 4, :].bitcast(I32), in_=v_s[32 * q + 4 : 32 * q + 8, :].bitcast(I32)
-            )
         load_tab(1)
+        load_w1(0, 0, held("raw00", [P, 4, PASS], F32)[:])
+        for q in range(4):
+            nc.sync.dma_start(
+                out=w4_s[32 * q : 32 * q + 4, :, :].bitcast(I32),
+                in_=w4_scales[:, 4 * q : 4 * q + 4, :].rearrange("a r c -> r a c").bitcast(I32),
+            )
         nc.sync.dma_start(
             out=w4_w[:].bitcast(I32), in_=w4_words.rearrange("a p c -> p a c").bitcast(I32)
         )
-        nc.sync.dma_start(out=gain_rows[0:MT, :], in_=gain.rearrange("(b p) -> b p", p=P))
+        nc.vector.tensor_copy(v_s[:], tab_s[:].indirect(idx[:]))
+        nc.sync.dma_start(out=v_s1[0 : P - 4, :].bitcast(I32), in_=v_s[4:P, :].bitcast(I32))
 
-        def load_route(q):
-            route_sb[q] = keep.tile([P, 4, S], F32, name="route_sb", tag="stream", bufs=2)
+        def load_route(q, tag):
+            route_sb[q] = keep.tile([P, 4, S], F32, name="route_sb%d" % q, tag=tag, align_bytes=64)
             nc.sync.dma_start(
                 out=route_sb[q][:], in_=route[4 * q * P : (4 * q + 4) * P, :].rearrange("(b p) j -> p b j", p=P)
             )
 
         def gather_victims(a, half):
-            tag = "shared%d1" % half if a == 1 else "v2_w0%d" % half
+            tag = ("w1_bf01", "late1")[a] if half == 1 else "v2_w%d%d" % (a, half)
             v2_w[a, half] = keep.tile([P, S2 // 2], U32, name="v2_w%d%d" % (a, half), tag=tag, align_bytes=64)
             gather_words(v2_w[a, half][:], a, idx2[:, half * S2 // 32 : (half + 1) * S2 // 32])
 
@@ -147,16 +144,19 @@ def tile_list_harness_crosstalk_match_kernel(
 
         gather_victim_scales(0)
         gather_victim_scales(1)
-        cast_w1(nc.scalar.copy, 0, 0, 0, PASS)
-        load_w1(1, 0)
+        raw_mid = stream.tile([P, 4, PASS], F32, name="raw10", offset=0)
+        raw_pair = stream.tile([P, 2, 4, PASS], F32, name="raw_pair", offset=CHUNK)
+        load_w1(0, 1, raw_pair[:, 0])
+        load_w1(1, 0, raw_mid[:])
+        load_w1(1, 1, raw_pair[:, 1])
         gather_words(v_w[0][:], 0, idx[:])
         gather_victims(0, 0)
-        quant_w1(0, 0)
-        gather_victims(0, 1)
-        cast_w1(nc.scalar.copy, 0, 1, 0, PASS)
-        load_w1(1, 1)
         gather_words(v_w[1][:], 1, idx[:])
-        quant_w1(0, 1)
+        cast_w1(nc.scalar.copy, 0, 0, 0, PASS)
+        load_route(0, "raw00")
+        quant_w1(0, 0)
+        load_route(1, "w1_bf00")
+        gather_victims(1, 0)
 
         v_planes = [v_s, v_s1]
         parked = {}
@@ -181,13 +181,17 @@ def tile_list_harness_crosstalk_match_kernel(
             )
 
         def park(weight, blk):
+            if blk == 0:
+                parked[blk] = held("parked0", [P, JT, PASS], F32)
+            else:
+                parked[blk] = stream.tile([P, JT, PASS], F32, name="parked1", offset=0)
             for jt in range(JT):
-                bank = psum.tile([P, PASS], F32, name="bank", tag="g")
-                product(bank, weight, blk, jt, 1, True)
-                product(bank, weight, blk, jt, 0, False)
-                parked[blk, jt] = held("parked%d%d" % (blk, jt), [P, PASS], F32)
+                tag = "a" if blk == 0 else "g"
+                bank = psum.tile([P, PASS], F32, name="bank", tag=tag, bufs=4 if tag == "a" else 2)
+                product(bank, weight, blk, jt, 0, True)
+                product(bank, weight, blk, jt, 1, False)
                 nc.scalar.copy(
-                    out=parked[blk, jt][:].rearrange("j (u p e) -> j u p e", u=2, e=2),
+                    out=parked[blk][:, jt, :].rearrange("j (u p e) -> j u p e", u=2, e=2),
                     in_=bank[:].rearrange("j (p u e) -> j u p e", u=2, e=2),
                 )
 
@@ -201,55 +205,56 @@ def tile_list_harness_crosstalk_match_kernel(
                 nc.vector.tensor_tensor(
                     out=h_t[blk, jt][:].rearrange("j (u p e) -> j u p e", u=2, e=2),
                     in0=banks[jt][:].rearrange("j (p u e) -> j u p e", u=2, e=2),
-                    in1=parked[blk, jt][:].rearrange("j (u p e) -> j u p e", u=2, e=2),
+                    in1=parked[blk][:, jt, :].rearrange("j (u p e) -> j u p e", u=2, e=2),
                     op=ALU.min,
                 )
 
         h_w = [held("h_w%d" % a, [P, S], U32) for a in range(PASSES)]
         h_s = [held("h_s%d" % a, [P, S], U8) for a in range(PASSES)]
-        h_bf = [held("h_bf%d" % a, [P, 4 * S], BF16) for a in range(PASSES)]
+        h_bf = {}
 
         def turn_h(blk):
+            tag = "h_bf0" if blk == 0 else "late1"
+            h_bf[blk] = keep.tile([P, 4 * S], BF16, name="h_bf%d" % blk, tag=tag, align_bytes=64)
             words_out = h_bf[blk][:].bitcast(F32)
-            for half in range(2):
-                bank = psum.tile([P, 2, 2, P], F32, name="tbank", tag="g")
-                for s in range(2):
-                    words = h_t[blk, 2 * half + s][:].bitcast(F32)
-                    for u in range(2):
-                        nc.tensor.transpose(bank[:, s, u, :], words[:, u * P : (u + 1) * P], ident[:])
+            for jt in range(JT):
+                bank = psum.tile([P, 2, P], F32, name="tbank", tag="gt"[blk], bufs=2)
+                words = h_t[blk, jt][:].bitcast(F32)
+                for u in range(2):
+                    nc.tensor.transpose(bank[:, u, :], words[:, u * P : (u + 1) * P], ident[:])
                 nc.scalar.copy(
-                    out=words_out[:, half * PASS : (half + 1) * PASS].rearrange("p (s j u) -> p s j u", s=2, u=2),
-                    in_=bank[:].rearrange("p s u j -> p s j u"),
+                    out=words_out[:, jt * 2 * P : (jt + 1) * 2 * P].rearrange("p (j u) -> p j u", u=2),
+                    in_=bank[:].rearrange("p u j -> p j u"),
                 )
 
         def quant_h(blk):
             nc.vector.quantize_mx(out=h_w[blk][:].bitcast(FP8X4), scales=h_s[blk][:], in_=h_bf[blk][:])
 
-        park("w1", 0)
-        gather_victims(1, 0)
-        meet("w4", 0)
-        park("w4", 1)
-        cast_w1(nc.vector.tensor_copy, 1, 0, 0, PASS)
-        load_route(0)
+        park("w4", 0)
+        cast_w1(nc.vector.tensor_copy, 0, 1, 0, PASS)
+        quant_w1(0, 1)
+        gather_victims(0, 1)
+        meet("w1", 0)
+        cast_w1(nc.scalar.copy, 1, 0, 0, PASS)
         quant_w1(1, 0)
-        cast_w1(nc.vector.tensor_copy, 1, 1, 0, SPLIT)
-        cast_w1(nc.scalar.copy, 1, 1, SPLIT, PASS)
-        load_route(1)
-        quant_w1(1, 1)
-        gather_victims(1, 1)
+        park("w4", 1)
         turn_h(0)
+        cast_w1(nc.vector.tensor_copy, 1, 1, 0, PASS)
+        quant_w1(1, 1)
         quant_h(0)
         meet("w1", 1)
-        turn_h(1)
-        gbank = psum.tile([P, PASS], F32, name="gbank", tag="g")
+        gbank = psum.tile([P, PASS], F32, name="gbank", tag="t", bufs=2)
         nc.tensor.transpose(gbank[:, 0:P], gain_rows[:], ident[:])
         nc.scalar.copy(out=gain_sb[:], in_=gbank[:, 0:MT])
+        turn_h(1)
         quant_h(1)
+        gather_victims(1, 1)
 
         stage = {}
 
         def match(i):
-            e = psum.tile([P, S], F32, name="e", tag="a" if i % 2 else "g")
+            tag = ("g", "g", "a", "a", "a", "a", "t", "t")[i]
+            e = psum.tile([P, S], F32, name="e", tag=tag, bufs=4 if tag == "a" else 2)
             cols = slice(i * P, (i + 1) * P)
             for a in range(PASSES):
                 nc.tensor.matmul_mx(
@@ -262,7 +267,7 @@ def tile_list_harness_crosstalk_match_kernel(
                     stop=(a == PASSES - 1),
                 )
             whole = ring.tile([P, S], I32, name="whole")
-            if i < 6:
+            if i in ON_SCALAR:
                 nc.scalar.activation(out=whole[:].bitcast(U32), in_=e[:], func=ACT.Copy, scale=1.0 / TWO_PI, bias=TURNS)
             else:
                 nc.vector.tensor_scalar(whole[:], e[:], 1.0 / TWO_PI, TURNS, ALU.mult, ALU.add)
@@ -273,27 +278,41 @@ def tile_list_harness_crosstalk_match_kernel(
             frac = ring.tile([P, S], F32, name="frac")
             nc.vector.scalar_tensor_tensor(frac[:], e[:], 1.0 / TWO_PI, whole[:], ALU.mult, ALU.subtract)
             size = ring.tile([P, S], F32, name="size")
+            nc.scalar.activation(out=size[:], in_=frac[:], func=ACT.Abs, bias=bias_turns[:])
+            stage[i] = (frac, size)
+
+        def pieces(i):
+            return [slice(0, S // 2), slice(S // 2, S)] if i == MT - 1 else [slice(0, S)]
+
+        def trig(i):
+            frac, size = stage[i]
             cos_e = ring.tile([P, S], F32, name="cos_e")
             sin_e = ring.tile([P, S], F32, name="sin_e")
-            nc.scalar.activation(out=size[:], in_=frac[:], func=ACT.Abs, bias=bias_turns[:])
-            nc.scalar.activation(out=sin_e[:], in_=frac[:], func=ACT.Sin, scale=TWO_PI, bias=bias_sin[:])
-            nc.scalar.activation(out=cos_e[:], in_=size[:], func=ACT.Sin, scale=-TWO_PI, bias=bias_cos[:])
+            for cols in pieces(i):
+                nc.scalar.activation(out=cos_e[:, cols], in_=size[:, cols], func=ACT.Sin, scale=-TWO_PI, bias=bias_cos[:])
+                nc.scalar.activation(out=sin_e[:, cols], in_=frac[:, cols], func=ACT.Sin, scale=TWO_PI, bias=bias_sin[:])
             stage[i] = (sin_e, cos_e)
 
         def route_far(i):
             sin_e, cos_e = stage[i]
             far = ring.tile([P, S], F32, name="far")
-            nc.vector.tensor_tensor(out=far[:], in0=cos_e[:], in1=route_sb[i // 4][:, i % 4, :], op=ALU.mult)
+            for cols in pieces(i):
+                nc.vector.tensor_tensor(
+                    out=far[:, cols], in0=cos_e[:, cols], in1=route_sb[i // 4][:, i % 4, cols], op=ALU.mult
+                )
             stage[i] = (sin_e, far)
 
         def finish(i):
             sin_e, far = stage[i]
             result = ring.tile([P, S], F32, name="result")
-            nc.vector.scalar_tensor_tensor(result[:], sin_e[:], gain_sb[:, i : i + 1], far[:], ALU.mult, ALU.add)
-            nc.sync.dma_start(out=out[i * P : (i + 1) * P, :], in_=result[:])
+            for cols in pieces(i):
+                nc.vector.scalar_tensor_tensor(
+                    result[:, cols], sin_e[:, cols], gain_sb[:, i : i + 1], far[:, cols], ALU.mult, ALU.add
+                )
+                nc.sync.dma_start(out=out[i * P : (i + 1) * P, cols], in_=result[:, cols])
 
-        steps = ((match, 0), (reduce_angle, 1), (route_far, 2), (finish, 3))
+        steps = ((reduce_angle, 1), (trig, 2), (route_far, 2), (finish, 3), (match, 0))
         for tick in range(MT + 4):
-            for step, lag in reversed(steps):
+            for step, lag in steps:
                 if 0 <= tick - lag < MT:
                     step(tick - lag)

@@ -24,6 +24,7 @@ PASSES = K // PASS
 JT = S // P
 MT = S2 // P
 TURNS = 16.0
+SPLIT = 288
 CHUNK = 4 * PASS * 4
 ON_SCALAR = (0, 1, 2, 3)
 TWO_PI = 2.0 * math.pi
@@ -60,8 +61,12 @@ def tile_list_harness_crosstalk_match_kernel(
         w1_s = {}
         for blk in range(PASSES):
             for a in range(PASSES):
-                tag = "w1_bf%d%d" % (blk, a)
-                w1_bf[blk, a] = keep.tile([P, 4 * PASS], BF16, name="w1_bf%d%d" % (blk, a), tag=tag, align_bytes=64)
+                if blk != a:
+                    w1_bf[blk, a] = stream.tile(
+                        [P, 4 * PASS], BF16, name="w1_bf%d%d" % (blk, a), offset=2 * CHUNK + blk * CHUNK // 2, align_bytes=64
+                    )
+                else:
+                    w1_bf[blk, a] = held("w1_bf%d%d" % (blk, a), [P, 4 * PASS], BF16)
                 w1_w[blk, a] = held("w1_w%d%d" % (blk, a), [P, PASS], U32)
                 w1_s[blk, a] = held("w1_s%d%d" % (blk, a), [P, PASS], U8)
         route_sb = {}
@@ -125,15 +130,20 @@ def tile_list_harness_crosstalk_match_kernel(
         nc.vector.tensor_copy(v_s[:], tab_s[:].indirect(idx[:]))
         nc.sync.dma_start(out=v_s1[0 : P - 4, :].bitcast(I32), in_=v_s[4:P, :].bitcast(I32))
 
-        def load_route(q, tag):
-            route_sb[q] = keep.tile([P, 4, S], F32, name="route_sb%d" % q, tag=tag, align_bytes=64)
+        def load_route(q, tile):
+            route_sb[q] = tile
             nc.sync.dma_start(
                 out=route_sb[q][:], in_=route[4 * q * P : (4 * q + 4) * P, :].rearrange("(b p) j -> p b j", p=P)
             )
 
         def gather_victims(a, half):
-            tag = ("w1_bf01", "late1")[a] if half == 1 else "v2_w%d%d" % (a, half)
-            v2_w[a, half] = keep.tile([P, S2 // 2], U32, name="v2_w%d%d" % (a, half), tag=tag, align_bytes=64)
+            name = "v2_w%d%d" % (a, half)
+            if half == 0:
+                v2_w[a, half] = held(name, [P, S2 // 2], U32)
+            else:
+                v2_w[a, half] = stream.tile(
+                    [P, S2 // 2], U32, name=name, offset=2 * CHUNK + a * CHUNK // 4, align_bytes=64
+                )
             gather_words(v2_w[a, half][:], a, idx2[:, half * S2 // 32 : (half + 1) * S2 // 32])
 
         def gather_victim_scales(half):
@@ -145,17 +155,16 @@ def tile_list_harness_crosstalk_match_kernel(
         gather_victim_scales(0)
         gather_victim_scales(1)
         raw_mid = stream.tile([P, 4, PASS], F32, name="raw10", offset=0)
-        raw_pair = stream.tile([P, 2, 4, PASS], F32, name="raw_pair", offset=CHUNK)
-        load_w1(0, 1, raw_pair[:, 0])
+        raw_low = stream.tile([P, 4, PASS], F32, name="raw01", offset=CHUNK)
+        load_w1(0, 1, raw_low[:])
         load_w1(1, 0, raw_mid[:])
-        load_w1(1, 1, raw_pair[:, 1])
         gather_words(v_w[0][:], 0, idx[:])
         gather_victims(0, 0)
         gather_words(v_w[1][:], 1, idx[:])
         cast_w1(nc.scalar.copy, 0, 0, 0, PASS)
-        load_route(0, "raw00")
+        load_w1(1, 1, keep.tile([P, 4, PASS], F32, name="raw11", tag="raw00", align_bytes=64)[:])
         quant_w1(0, 0)
-        load_route(1, "w1_bf00")
+        load_route(0, keep.tile([P, 4, S], F32, name="route0", tag="w1_bf00", align_bytes=64))
         gather_victims(1, 0)
 
         v_planes = [v_s, v_s1]
@@ -180,45 +189,54 @@ def tile_list_harness_crosstalk_match_kernel(
                 stop=not first,
             )
 
-        def park(weight, blk):
-            if blk == 0:
-                parked[blk] = held("parked0", [P, JT, PASS], F32)
-            else:
-                parked[blk] = stream.tile([P, JT, PASS], F32, name="parked1", offset=0)
-            for jt in range(JT):
-                tag = "a" if blk == 0 else "g"
+        def park(weight, blk, tiles):
+            for jt in tiles:
+                name = "parked%d%d" % (blk, jt)
+                if blk == 1:
+                    parked[blk, jt] = stream.tile([P, PASS], F32, name=name, offset=jt * CHUNK // 4)
+                else:
+                    parked[blk, jt] = held(name, [P, PASS], F32)
+                tag = "a" if blk == 0 else "gt"[jt // 2]
                 bank = psum.tile([P, PASS], F32, name="bank", tag=tag, bufs=4 if tag == "a" else 2)
                 product(bank, weight, blk, jt, 0, True)
                 product(bank, weight, blk, jt, 1, False)
                 nc.scalar.copy(
-                    out=parked[blk][:, jt, :].rearrange("j (u p e) -> j u p e", u=2, e=2),
+                    out=parked[blk, jt][:].rearrange("j (u p e) -> j u p e", u=2, e=2),
                     in_=bank[:].rearrange("j (p u e) -> j u p e", u=2, e=2),
                 )
 
-        def meet(weight, blk):
+        def open_sums(weight, blk):
             banks = [psum.tile([P, PASS], F32, name="abank", tag="a") for jt in range(JT)]
-            for a in range(PASSES):
-                for jt in range(JT):
-                    product(banks[jt], weight, blk, jt, a, a == 0)
             for jt in range(JT):
-                h_t[blk, jt] = held("h_t%d%d" % (blk, jt), [P, PASS], BF16)
+                product(banks[jt], weight, blk, jt, 0, True)
+            return banks
+
+        def close_sums(weight, blk, banks):
+            for jt in range(JT):
+                product(banks[jt], weight, blk, jt, 1, False)
+
+        def meet(blk, banks):
+            for jt in range(JT):
+                name = "h_t%d%d" % (blk, jt)
+                if blk == 0:
+                    h_t[blk, jt] = stream.tile([P, PASS], BF16, name=name, offset=5 * CHUNK // 2 + jt * CHUNK // 8)
+                else:
+                    h_t[blk, jt] = held(name, [P, PASS], BF16)
                 nc.vector.tensor_tensor(
                     out=h_t[blk, jt][:].rearrange("j (u p e) -> j u p e", u=2, e=2),
                     in0=banks[jt][:].rearrange("j (p u e) -> j u p e", u=2, e=2),
-                    in1=parked[blk][:, jt, :].rearrange("j (u p e) -> j u p e", u=2, e=2),
+                    in1=parked[blk, jt][:].rearrange("j (u p e) -> j u p e", u=2, e=2),
                     op=ALU.min,
                 )
 
-        h_w = [held("h_w%d" % a, [P, S], U32) for a in range(PASSES)]
+        h_w = {}
         h_s = [held("h_s%d" % a, [P, S], U8) for a in range(PASSES)]
         h_bf = {}
 
-        def turn_h(blk):
-            tag = "h_bf0" if blk == 0 else "late1"
-            h_bf[blk] = keep.tile([P, 4 * S], BF16, name="h_bf%d" % blk, tag=tag, align_bytes=64)
+        def turn_h(blk, tiles):
             words_out = h_bf[blk][:].bitcast(F32)
-            for jt in range(JT):
-                bank = psum.tile([P, 2, P], F32, name="tbank", tag="gt"[blk], bufs=2)
+            for jt in tiles:
+                bank = psum.tile([P, 2, P], F32, name="tbank", tag="gt"[jt % 2], bufs=2)
                 words = h_t[blk, jt][:].bitcast(F32)
                 for u in range(2):
                     nc.tensor.transpose(bank[:, u, :], words[:, u * P : (u + 1) * P], ident[:])
@@ -228,27 +246,39 @@ def tile_list_harness_crosstalk_match_kernel(
                 )
 
         def quant_h(blk):
+            if blk == 0:
+                h_w[blk] = stream.tile([P, S], U32, name="h_w0", offset=3 * CHUNK // 4, align_bytes=64)
+            else:
+                h_w[blk] = held("h_w1", [P, S], U32)
             nc.vector.quantize_mx(out=h_w[blk][:].bitcast(FP8X4), scales=h_s[blk][:], in_=h_bf[blk][:])
 
-        park("w4", 0)
-        cast_w1(nc.vector.tensor_copy, 0, 1, 0, PASS)
-        quant_w1(0, 1)
-        gather_victims(0, 1)
-        meet("w1", 0)
-        cast_w1(nc.scalar.copy, 1, 0, 0, PASS)
-        quant_w1(1, 0)
-        park("w4", 1)
-        turn_h(0)
-        cast_w1(nc.vector.tensor_copy, 1, 1, 0, PASS)
-        quant_w1(1, 1)
-        quant_h(0)
-        meet("w1", 1)
         gbank = psum.tile([P, PASS], F32, name="gbank", tag="t", bufs=2)
         nc.tensor.transpose(gbank[:, 0:P], gain_rows[:], ident[:])
         nc.scalar.copy(out=gain_sb[:], in_=gbank[:, 0:MT])
-        turn_h(1)
-        quant_h(1)
+        park("w4", 0, range(JT))
+        banks = open_sums("w1", 0)
+        cast_w1(nc.vector.tensor_copy, 0, 1, 0, PASS)
+        load_route(1, stream.tile([P, 4, S], F32, name="route1", offset=CHUNK))
+        quant_w1(0, 1)
+        gather_victims(0, 1)
         gather_victims(1, 1)
+        close_sums("w1", 0, banks)
+        cast_w1(nc.scalar.copy, 1, 0, 0, PASS)
+        quant_w1(1, 0)
+        meet(0, banks)
+        park("w4", 1, range(JT))
+        banks = open_sums("w1", 1)
+        cast_w1(nc.vector.tensor_copy, 1, 1, 0, SPLIT)
+        cast_w1(nc.scalar.copy, 1, 1, SPLIT, PASS)
+        quant_w1(1, 1)
+        close_sums("w1", 1, banks)
+        meet(1, banks)
+        h_bf[0] = held("h_bf0", [P, 4 * S], BF16)
+        turn_h(0, range(JT))
+        quant_h(0)
+        h_bf[1] = held("h_bf1", [P, 4 * S], BF16)
+        turn_h(1, range(JT))
+        quant_h(1)
 
         stage = {}
 
@@ -256,15 +286,16 @@ def tile_list_harness_crosstalk_match_kernel(
             tag = ("g", "g", "a", "a", "a", "a", "t", "t")[i]
             e = psum.tile([P, S], F32, name="e", tag=tag, bufs=4 if tag == "a" else 2)
             cols = slice(i * P, (i + 1) * P)
-            for a in range(PASSES):
+            order = (0, 1) if i < 2 else (1, 0)
+            for a in order:
                 nc.tensor.matmul_mx(
                     out=e[:],
                     lhsT=v2_w[a, i // 4][:, (i % 4) * P : (i % 4 + 1) * P].bitcast(FP8X4),
                     lhsT_scale=v2_s[4 * a : P, cols],
                     rhs=h_w[a][:].bitcast(FP8X4),
                     rhs_scale=h_s[a][:],
-                    start=(a == 0),
-                    stop=(a == PASSES - 1),
+                    start=(a == order[0]),
+                    stop=(a == order[1]),
                 )
             whole = ring.tile([P, S], I32, name="whole")
             if i in ON_SCALAR:

@@ -79,15 +79,16 @@ def tile_list_harness_crosstalk_match_kernel(
         bias_turns = held("bias_turns", [P, 1], F32)
 
         nc.vector.memset(tab_s[:].bitcast(I32), 0)
+        nc.vector.memset(gain_rows[:], 0.0)
+        nc.scalar.dma_start(out=gain_rows[0:MT, :], in_=gain.rearrange("(b p) -> b p", p=P))
         nc.vector.memset(w4_s[:].rearrange("p a c -> p (a c)").bitcast(I32), 0)
         nc.vector.memset(v_s1[:].bitcast(I32), 0)
-        nc.gpsimd.memset(gain_rows[:], 0.0)
-        nc.gpsimd.dma_start(out=gain_rows[0:MT, :], in_=gain.rearrange("(b p) -> b p", p=P))
-        make_identity(nc, ident[:])
-        nc.gpsimd.memset(one[:], 1.0)
-        nc.gpsimd.memset(bias_turns[:], TURNS)
-        nc.gpsimd.tensor_scalar(bias_sin[:], one[:], TWO_PI * TURNS, 0.0, ALU.mult, ALU.add)
-        nc.gpsimd.tensor_scalar(bias_cos[:], one[:], 0.5 * math.pi, 0.0, ALU.mult, ALU.add)
+        nc.vector.memset(one[:], 1.0)
+        nc.vector.memset(bias_turns[:], TURNS)
+        nc.vector.tensor_scalar(bias_sin[:], one[:], TWO_PI * TURNS, None, ALU.mult)
+        nc.vector.tensor_scalar(bias_cos[:], one[:], 0.5 * math.pi, None, ALU.mult)
+        nc.vector.memset(ident[:], 0.0)
+        make_identity(nc, ident[:], nomemset=True)
 
         def load_w1(blk, a, tile):
             rows = w1[a * PASS : (a + 1) * PASS, blk * PASS : (blk + 1) * PASS]
@@ -128,7 +129,7 @@ def tile_list_harness_crosstalk_match_kernel(
             out=w4_w[:].bitcast(I32), in_=w4_words.rearrange("a p c -> p a c").bitcast(I32)
         )
         nc.vector.tensor_copy(v_s[:], tab_s[:].indirect(idx[:]))
-        nc.sync.dma_start(out=v_s1[0 : P - 4, :].bitcast(I32), in_=v_s[4:P, :].bitcast(I32))
+        nc.sync.dma_start(out=v_s1[0:112, :].bitcast(I32), in_=v_s[4:116, :].bitcast(I32))
 
         def load_route(q, tile):
             route_sb[q] = tile
@@ -252,9 +253,6 @@ def tile_list_harness_crosstalk_match_kernel(
                 h_w[blk] = held("h_w1", [P, S], U32)
             nc.vector.quantize_mx(out=h_w[blk][:].bitcast(FP8X4), scales=h_s[blk][:], in_=h_bf[blk][:])
 
-        gbank = psum.tile([P, PASS], F32, name="gbank", tag="t", bufs=2)
-        nc.tensor.transpose(gbank[:, 0:P], gain_rows[:], ident[:])
-        nc.scalar.copy(out=gain_sb[:], in_=gbank[:, 0:MT])
         park("w4", 0, range(JT))
         banks = open_sums("w1", 0)
         cast_w1(nc.vector.tensor_copy, 0, 1, 0, PASS)
@@ -275,6 +273,9 @@ def tile_list_harness_crosstalk_match_kernel(
         meet(1, banks)
         h_bf[0] = held("h_bf0", [P, 4 * S], BF16)
         turn_h(0, range(JT))
+        gbank = psum.tile([P, PASS], F32, name="gbank", tag="t", bufs=2)
+        nc.tensor.transpose(gbank[:, 0:P], gain_rows[:], ident[:])
+        nc.scalar.copy(out=gain_sb[:], in_=gbank[:, 0:MT])
         quant_h(0)
         h_bf[1] = held("h_bf1", [P, 4 * S], BF16)
         turn_h(1, range(JT))

@@ -84,6 +84,8 @@ def tile_list_harness_crosstalk_match_kernel(
         nc.vector.memset(w4_s[:].rearrange("p a c -> p (a c)").bitcast(I32), 0)
         nc.vector.memset(v_s1[:].bitcast(I32), 0)
         nc.vector.memset(one[:], 1.0)
+        warm = held("warm", [P, 1], F32)
+        nc.scalar.activation(out=warm[:], in_=one[:], func=ACT.Sin)
         nc.vector.memset(bias_turns[:], TURNS)
         nc.vector.tensor_scalar(bias_sin[:], one[:], TWO_PI * TURNS, None, ALU.mult)
         nc.vector.tensor_scalar(bias_cos[:], one[:], 0.5 * math.pi, None, ALU.mult)

import math
from contextlib import ExitStack

import concourse.mybir as mybir
from concourse.masks import make_identity

K, T, S, S2 = 1024, 2048, 512, 1024
FLOPS = 2 * K * K * S * 2 + 2 * K * S2 * S

F32 = mybir.dt.float32
BF16 = mybir.dt.bfloat16
I32 = mybir.dt.int32
U32 = mybir.dt.uint32
U16 = mybir.dt.uint16
U8 = mybir.dt.uint8
FP8X4 = mybir.dt.float8_e4m3fn_x4
FP4X4 = mybir.dt.float4_e2m1fn_x4
ALU = mybir.AluOpType
ACT = mybir.ActivationFunctionType

P = 128
PASS = 512
PASSES = K // PASS
JT = S // P
MT = S2 // P
TURNS = 16.0
SPLIT = 288
CHUNK = 4 * PASS * 4
ON_SCALAR = (0, 1, 2, 3)
TWO_PI = 2.0 * math.pi


def tile_list_harness_crosstalk_match_kernel(
    tc, tab_words, tab_scales, w1, w4_words, w4_scales, gain, route, offs, offs2, out
):
    nc = tc.nc
    with ExitStack() as ctx:
        lists = ctx.enter_context(tc.tile_pool(name="lists", bufs=1))
        keep = ctx.enter_context(tc.tile_pool(name="keep", bufs=1))
        stream = ctx.enter_context(tc.tile_pool(name="stream", bufs=1))
        ring = ctx.enter_context(tc.tile_pool(name="ring", bufs=5))
        psum = ctx.enter_context(tc.psum_pool(name="psum", bufs=4))

        def held(name, shape, dtype):
            return keep.tile(shape, dtype, name=name, align_bytes=64)

        idx = lists.tile([P, S // 16], U16, name="idx")
        idx2 = lists.tile([P, S2 // 16], U16, name="idx2")
        tab_s = stream.tile([P, T], U8, name="tab_s", offset=CHUNK - T // 2)
        tab_w = [held("tab_w%d" % a, [P, T], I32) for a in range(PASSES)]
        w4_w = held("w4_w", [P, PASSES, 2 * K], U8)
        w4_s = held("w4_s", [P, PASSES, K], U8)
        v_w = [held("v_w%d" % a, [P, S], U32) for a in range(PASSES)]
        v_s = held("v_s", [P, S], U8)
        v_s1 = held("v_s1", [P, S], U8)
        v2_w = {}
        v2_s = held("v2_s", [P, S2], U8)
        raw = {}
        w1_bf = {}
        w1_w = {}
        w1_s = {}
        for blk in range(PASSES):
            for a in range(PASSES):
                if blk != a:
                    w1_bf[blk, a] = stream.tile(
                        [P, 4 * PASS], BF16, name="w1_bf%d%d" % (blk, a), offset=2 * CHUNK + blk * CHUNK // 2, align_bytes=64
                    )
                else:
                    w1_bf[blk, a] = held("w1_bf%d%d" % (blk, a), [P, 4 * PASS], BF16)
                w1_w[blk, a] = held("w1_w%d%d" % (blk, a), [P, PASS], U32)
                w1_s[blk, a] = held("w1_s%d%d" % (blk, a), [P, PASS], U8)
        route_sb = {}
        ident = held("ident", [P, P], F32)
        gain_rows = held("gain_rows", [P, P], F32)
        gain_sb = held("gain_sb", [P, MT], F32)
        one = held("one", [P, 1], F32)
        bias_sin = held("bias_sin", [P, 1], F32)
        bias_cos = held("bias_cos", [P, 1], F32)
        bias_turns = held("bias_turns", [P, 1], F32)

        nc.vector.memset(tab_s[:].bitcast(I32), 0)
        nc.vector.memset(gain_rows[:], 0.0)
        nc.scalar.dma_start(out=gain_rows[0:MT, :], in_=gain.rearrange("(b p) -> b p", p=P))
        nc.vector.memset(w4_s[:].rearrange("p a c -> p (a c)").bitcast(I32), 0)
        nc.vector.memset(v_s1[:].bitcast(I32), 0)
        nc.vector.memset(one[:], 1.0)
        warm = held("warm", [P, 1], F32)
        nc.scalar.activation(out=warm[:], in_=one[:], func=ACT.Sin)
        nc.vector.memset(bias_turns[:], TURNS)
        nc.vector.tensor_scalar(bias_sin[:], one[:], TWO_PI * TURNS, None, ALU.mult)
        nc.vector.tensor_scalar(bias_cos[:], one[:], 0.5 * math.pi, None, ALU.mult)
        nc.vector.memset(ident[:], 0.0)
        make_identity(nc, ident[:], nomemset=True)

        def load_w1(blk, a, tile):
            rows = w1[a * PASS : (a + 1) * PASS, blk * PASS : (blk + 1) * PASS]
            raw[blk, a] = tile
            nc.sync.dma_start(out=tile, in_=rows.rearrange("(p j) c -> p j c", j=4))

        def load_tab(a):
            nc.sync.dma_start(out=tab_w[a][:], in_=tab_words[a].rearrange("p t i -> p (t i)").bitcast(I32))

        def cast_w1(copy, blk, a, first, last):
            copy(
                out=w1_bf[blk, a][:, 4 * first : 4 * last].rearrange("p (c i j) -> p c j i", i=4, j=4),
                in_=raw[blk, a][:, :, first:last].rearrange("p j (c i) -> p c j i", i=4),
            )

        def quant_w1(blk, a):
            nc.vector.quantize_mx(out=w1_w[blk, a][:].bitcast(FP8X4), scales=w1_s[blk, a][:], in_=w1_bf[blk, a][:])

        def gather_words(dst, a, offsets):
            nc.vector.tensor_copy(dst, tab_w[a][:].bitcast(U32).indirect(offsets))

        nc.sync.dma_start(idx[:], offs)
        for q in range(4):
            nc.sync.dma_start(
                out=tab_s[32 * q : 32 * q + 8, :].bitcast(I32),
                in_=tab_scales[:, 4 * q : 4 * q + 4, :].bitcast(I32),
            )
        nc.sync.dma_start(idx2[:], offs2)
        load_tab(0)
        load_tab(1)
        load_w1(0, 0, held("raw00", [P, 4, PASS], F32)[:])
        for q in range(4):
            nc.sync.dma_start(
                out=w4_s[32 * q : 32 * q + 4, :, :].bitcast(I32),
                in_=w4_scales[:, 4 * q : 4 * q + 4, :].rearrange("a r c -> r a c").bitcast(I32),
            )
        nc.sync.dma_start(
            out=w4_w[:].bitcast(I32), in_=w4_words.rearrange("a p c -> p a c").bitcast(I32)
        )
        nc.vector.tensor_copy(v_s[:], tab_s[:].indirect(idx[:]))
        nc.sync.dma_start(out=v_s1[0:112, :].bitcast(I32), in_=v_s[4:116, :].bitcast(I32))

        def load_route(q, tile):
            route_sb[q] = tile
            nc.sync.dma_start(
                out=route_sb[q][:], in_=route[4 * q * P : (4 * q + 4) * P, :].rearrange("(b p) j -> p b j", p=P)
            )

        def gather_victims(a, half):
            name = "v2_w%d%d" % (a, half)
            if half == 0:
                v2_w[a, half] = held(name, [P, S2 // 2], U32)
            else:
                v2_w[a, half] = stream.tile(
                    [P, S2 // 2], U32, name=name, offset=2 * CHUNK + a * CHUNK // 4, align_bytes=64
                )
            gather_words(v2_w[a, half][:], a, idx2[:, half * S2 // 32 : (half + 1) * S2 // 32])

        def gather_victim_scales(half):
            nc.vector.tensor_copy(
                v2_s[:, half * S2 // 2 : (half + 1) * S2 // 2],
                tab_s[:].indirect(idx2[:, half * S2 // 32 : (half + 1) * S2 // 32]),
            )

        gather_victim_scales(0)
        gather_victim_scales(1)
        raw_mid = stream.tile([P, 4, PASS], F32, name="raw10", offset=0)
        raw_low = stream.tile([P, 4, PASS], F32, name="raw01", offset=CHUNK)
        load_w1(0, 1, raw_low[:])
        load_w1(1, 0, raw_mid[:])
        gather_words(v_w[0][:], 0, idx[:])
        gather_victims(0, 0)
        gather_words(v_w[1][:], 1, idx[:])
        cast_w1(nc.scalar.copy, 0, 0, 0, PASS)
        load_w1(1, 1, keep.tile([P, 4, PASS], F32, name="raw11", tag="raw00", align_bytes=64)[:])
        quant_w1(0, 0)
        load_route(0, keep.tile([P, 4, S], F32, name="route0", tag="w1_bf00", align_bytes=64))
        gather_victims(1, 0)

        v_planes = [v_s, v_s1]
        parked = {}
        h_t = {}

        def product(bank, weight, blk, jt, a, first):
            cols = slice(jt * P, (jt + 1) * P)
            if weight == "w4":
                rhs = w4_w[:, a, 2 * blk * PASS : 2 * (blk + 1) * PASS].bitcast(FP4X4)
                rhs_scale = w4_s[:, a, blk * PASS : (blk + 1) * PASS]
            else:
                rhs = w1_w[blk, a][:].bitcast(FP8X4)
                rhs_scale = w1_s[blk, a][:]
            nc.tensor.matmul_mx(
                out=bank[:],
                lhsT=v_w[a][:, cols].bitcast(FP8X4),
                lhsT_scale=v_planes[a][:, cols] if weight == "w4" else v_s[4 * a : P, cols],
                rhs=rhs,
                rhs_scale=rhs_scale,
                start=first,
                stop=not first,
            )

        def park(weight, blk, tiles):
            for jt in tiles:
                name = "parked%d%d" % (blk, jt)
                if blk == 1:
                    parked[blk, jt] = stream.tile([P, PASS], F32, name=name, offset=jt * CHUNK // 4)
                else:
                    parked[blk, jt] = held(name, [P, PASS], F32)
                tag = "a" if blk == 0 else "gt"[jt // 2]
                bank = psum.tile([P, PASS], F32, name="bank", tag=tag, bufs=4 if tag == "a" else 2)
                product(bank, weight, blk, jt, 0, True)
                product(bank, weight, blk, jt, 1, False)
                nc.scalar.copy(
                    out=parked[blk, jt][:].rearrange("j (u p e) -> j u p e", u=2, e=2),
                    in_=bank[:].rearrange("j (p u e) -> j u p e", u=2, e=2),
                )

        def open_sums(weight, blk):
            banks = [psum.tile([P, PASS], F32, name="abank", tag="a") for jt in range(JT)]
            for jt in range(JT):
                product(banks[jt], weight, blk, jt, 0, True)
            return banks

        def close_sums(weight, blk, banks):
            for jt in range(JT):
                product(banks[jt], weight, blk, jt, 1, False)

        def meet(blk, banks):
            for jt in range(JT):
                name = "h_t%d%d" % (blk, jt)
                if blk == 0:
                    h_t[blk, jt] = stream.tile([P, PASS], BF16, name=name, offset=5 * CHUNK // 2 + jt * CHUNK // 8)
                else:
                    h_t[blk, jt] = held(name, [P, PASS], BF16)
                nc.vector.tensor_tensor(
                    out=h_t[blk, jt][:].rearrange("j (u p e) -> j u p e", u=2, e=2),
                    in0=banks[jt][:].rearrange("j (p u e) -> j u p e", u=2, e=2),
                    in1=parked[blk, jt][:].rearrange("j (u p e) -> j u p e", u=2, e=2),
                    op=ALU.min,
                )

        h_w = {}
        h_s = [held("h_s%d" % a, [P, S], U8) for a in range(PASSES)]
        h_bf = {}

        def turn_h(blk, tiles):
            words_out = h_bf[blk][:].bitcast(F32)
            for jt in tiles:
                bank = psum.tile([P, 2, P], F32, name="tbank", tag="gt"[jt % 2], bufs=2)
                words = h_t[blk, jt][:].bitcast(F32)
                for u in range(2):
                    nc.tensor.transpose(bank[:, u, :], words[:, u * P : (u + 1) * P], ident[:])
                nc.scalar.copy(
                    out=words_out[:, jt * 2 * P : (jt + 1) * 2 * P].rearrange("p (j u) -> p j u", u=2),
                    in_=bank[:].rearrange("p u j -> p j u"),
                )

        def quant_h(blk):
            if blk == 0:
                h_w[blk] = stream.tile([P, S], U32, name="h_w0", offset=3 * CHUNK // 4, align_bytes=64)
            else:
                h_w[blk] = held("h_w1", [P, S], U32)
            nc.vector.quantize_mx(out=h_w[blk][:].bitcast(FP8X4), scales=h_s[blk][:], in_=h_bf[blk][:])

        park("w4", 0, range(JT))
        banks = open_sums("w1", 0)
        cast_w1(nc.vector.tensor_copy, 0, 1, 0, PASS)
        load_route(1, stream.tile([P, 4, S], F32, name="route1", offset=CHUNK))
        quant_w1(0, 1)
        gather_victims(0, 1)
        gather_victims(1, 1)
        close_sums("w1", 0, banks)
        cast_w1(nc.scalar.copy, 1, 0, 0, PASS)
        quant_w1(1, 0)
        meet(0, banks)
        park("w4", 1, range(JT))
        banks = open_sums("w1", 1)
        cast_w1(nc.vector.tensor_copy, 1, 1, 0, SPLIT)
        cast_w1(nc.scalar.copy, 1, 1, SPLIT, PASS)
        quant_w1(1, 1)
        close_sums("w1", 1, banks)
        meet(1, banks)
        h_bf[0] = held("h_bf0", [P, 4 * S], BF16)
        turn_h(0, range(JT))
        gbank = psum.tile([P, PASS], F32, name="gbank", tag="t", bufs=2)
        nc.tensor.transpose(gbank[:, 0:P], gain_rows[:], ident[:])
        nc.scalar.copy(out=gain_sb[:], in_=gbank[:, 0:MT])
        quant_h(0)
        h_bf[1] = held("h_bf1", [P, 4 * S], BF16)
        turn_h(1, range(JT))
        quant_h(1)

        stage = {}

        def match(i):
            tag = ("g", "g", "a", "a", "a", "a", "t", "t")[i]
            e = psum.tile([P, S], F32, name="e", tag=tag, bufs=4 if tag == "a" else 2)
            cols = slice(i * P, (i + 1) * P)
            order = (0, 1) if i < 2 else (1, 0)
            for a in order:
                nc.tensor.matmul_mx(
                    out=e[:],
                    lhsT=v2_w[a, i // 4][:, (i % 4) * P : (i % 4 + 1) * P].bitcast(FP8X4),
                    lhsT_scale=v2_s[4 * a : P, cols],
                    rhs=h_w[a][:].bitcast(FP8X4),
                    rhs_scale=h_s[a][:],
                    start=(a == order[0]),
                    stop=(a == order[1]),
                )
            whole = ring.tile([P, S], I32, name="whole")
            if i in ON_SCALAR:
                nc.scalar.activation(out=whole[:].bitcast(U32), in_=e[:], func=ACT.Copy, scale=1.0 / TWO_PI, bias=TURNS)
            else:
                nc.vector.tensor_scalar(whole[:], e[:], 1.0 / TWO_PI, TURNS, ALU.mult, ALU.add)
            stage[i] = (e, whole)

        def reduce_angle(i):
            e, whole = stage[i]
            frac = ring.tile([P, S], F32, name="frac")
            nc.vector.scalar_tensor_tensor(frac[:], e[:], 1.0 / TWO_PI, whole[:], ALU.mult, ALU.subtract)
            size = ring.tile([P, S], F32, name="size")
            nc.scalar.activation(out=size[:], in_=frac[:], func=ACT.Abs, bias=bias_turns[:])
            stage[i] = (frac, size)

        def pieces(i):
            return [slice(0, S // 2), slice(S // 2, S)] if i == MT - 1 else [slice(0, S)]

        def trig(i):
            frac, size = stage[i]
            cos_e = ring.tile([P, S], F32, name="cos_e")
            sin_e = ring.tile([P, S], F32, name="sin_e")
            for cols in pieces(i):
                nc.scalar.activation(out=cos_e[:, cols], in_=size[:, cols], func=ACT.Sin, scale=-TWO_PI, bias=bias_cos[:])
                nc.scalar.activation(out=sin_e[:, cols], in_=frac[:, cols], func=ACT.Sin, scale=TWO_PI, bias=bias_sin[:])
            stage[i] = (sin_e, cos_e)

        def route_far(i):
            sin_e, cos_e = stage[i]
            far = ring.tile([P, S], F32, name="far")
            for cols in pieces(i):
                nc.vector.tensor_tensor(
                    out=far[:, cols], in0=cos_e[:, cols], in1=route_sb[i // 4][:, i % 4, cols], op=ALU.mult
                )
            stage[i] = (sin_e, far)

        def finish(i):
            sin_e, far = stage[i]
            result = ring.tile([P, S], F32, name="result")
            for cols in pieces(i):
                nc.vector.scalar_tensor_tensor(
                    result[:, cols], sin_e[:, cols], gain_sb[:, i : i + 1], far[:, cols], ALU.mult, ALU.add
                )
                nc.sync.dma_start(out=out[i * P : (i + 1) * P, cols], in_=result[:, cols])

        steps = ((reduce_angle, 1), (trig, 2), (route_far, 2), (finish, 3), (match, 0))
        for tick in range(MT + 4):
            for step, lag in steps:
                if 0 <= tick - lag < MT:
                    step(tick - lag)
